import numpy as np, ml_dtypes
CORES = [2,34,66,98,130,162,194,226,258,290,322,354,386,418,450,482]
N = 16
WB, F = 1, 64
def setup_inputs(rng):
    return {"a": rng.standard_normal((N, 128, 128), dtype=np.float32).astype(ml_dtypes.bfloat16), "w": rng.standard_normal((N, 128, F), dtype=np.float32).astype(ml_dtypes.bfloat16)}
def setup_inputs_big(rng):
    d = setup_inputs(rng)
    for k in ("a", "w"): d[k] = (d[k].astype(np.float32) * 1024.0).astype(d[k].dtype)
    return d
def setup_inputs_small(rng):
    d = setup_inputs(rng)
    for k in ("a", "w"): d[k] = (d[k].astype(np.float32) * (1 / 1024.0)).astype(d[k].dtype)
    return d
def setup_inputs_apart(rng):
    d = setup_inputs(rng)
    f = (10.0 ** rng.permutation(np.linspace(-1.5, 1.5, N))).astype(np.float32).reshape(N, 1, 1)
    for k in ("a", "w"): d[k] = (d[k].astype(np.float32) * f).astype(d[k].dtype)
    return d
def reference(a, w):
    A, W = a.astype(np.float64), w.astype(np.float64)
    p = [A[j].T @ W[j] for j in range(N)]
    y = np.stack([sum(p[r - i] for i in range(WB + 1) if r - i >= 0) for r in range(N)])
    return {"y": y.astype(ml_dtypes.bfloat16 if a.dtype != np.float64 else np.float64)}

from concourse.mybir import AluOpType

SCRATCH = {
    "ab": ("sbuf", [128, 128], "bfloat16"),
    "wb": ("sbuf", [128, 64], "bfloat16"),
    "ps": ("psum", [128, 64], "float32"),
    "pb": ("sbuf", [128, 64], "bfloat16"),
    "land": ("sbuf", [128, 64], "bfloat16"),
    "yb": ("sbuf", [128, 64], "bfloat16"),
}
SEMAPHORES = ["ld", "mm", "cp", "arr", "sent", "sm", "st"]


def engines(mask):
    return bin(mask).count("1")


def rank_program(g, core, T, topo):
    rank = T.rank_of(core)
    if rank is None:
        return
    n = len(T.cores)
    s = T.sem
    nxt = T.cores[rank + 1] if rank + 1 < n else None
    prv = T.cores[rank - 1] if rank > 0 else None

    g.sync.dma_start(T.ab[:], T.a[:]).then_inc(s.ld, 16)
    g.scalar.dma_start(T.wb[:], T.w[:]).then_inc(s.ld, 16)

    g.tensor.wait_ge(s.ld, 32)
    g.tensor.matmul(T.ps[:], T.ab[:], T.wb[:], True, True).then_inc(s.mm, 1)
    g.vector.wait_ge(s.mm, 1)
    if nxt is not None:
        g.vector.tensor_copy(T.pb[:], T.ps[:]).then_inc(s.cp, 1)

        rid, pid = topo.addr(nxt, core)
        m = topo.mask(core, nxt)
        g.wait_ge(s.cp, 1)
        g.remote_dma(out_ap=T.land[:], in_ap=T.pb[:], remote_sem=s.arr, local_sem=s.sent,
                     pid=pid, routing_id=rid, dma_engine_mask=m)

    if prv is not None:
        g.vector.wait_ge(s.arr, engines(topo.mask(prv, core)))
        g.vector.tensor_tensor(T.yb[:], T.ps[:], T.land[:], AluOpType.add).then_inc(s.sm, 1)
        g.sync.wait_ge(s.sm, 1)
        g.sync.dma_start(T.y[:], T.yb[:]).then_inc(s.st, 16)
    else:
        g.sync.wait_ge(s.cp, 1)
        g.sync.dma_start(T.y[:], T.pb[:]).then_inc(s.st, 16)
    g.sync.wait_ge(s.st, 16)
    if nxt is not None:
        g.wait_ge(s.sent, engines(topo.mask(core, nxt)))
